import numpy as np
CORES = [71,199,95,223,103,231,111,239,119,247,127,255]
N = 12
def setup_inputs(rng):
    dy = rng.standard_normal((N, 128, N * 128), dtype=np.float32)
    dyt = np.concatenate([dy[:, :, 128 * j:128 * j + 128].transpose(0, 2, 1) for j in range(N)], axis=2)
    return {"x": rng.standard_normal((N, 128, 128), dtype=np.float32), "wt": rng.standard_normal((N, 128, 128), dtype=np.float32), "dy": dy, "dyt": dyt}
def setup_inputs_big(rng):
    d = setup_inputs(rng)
    for k in ("x", "wt", "dy", "dyt"): d[k] = (d[k].astype(np.float32) * 1024.0).astype(d[k].dtype)
    return d
def setup_inputs_small(rng):
    d = setup_inputs(rng)
    for k in ("x", "wt", "dy", "dyt"): d[k] = (d[k].astype(np.float32) * (1 / 1024.0)).astype(d[k].dtype)
    return d
def setup_inputs_apart(rng):
    d = setup_inputs(rng)
    f = (10.0 ** rng.permutation(np.linspace(-1.5, 1.5, N))).astype(np.float32).reshape(N, 1, 1)
    for k in ("x", "wt", "dy", "dyt"): d[k] = (d[k].astype(np.float32) * f).astype(d[k].dtype)
    return d
def tie_inputs(x):
    x = dict(x)
    x["dyt"] = np.concatenate([x["dy"][:, :, 128 * j:128 * j + 128].transpose(0, 2, 1) for j in range(N)], axis=2)
    return x
def reference(x, wt, dy, dyt):
    X, WT, DY, DYT = x.astype(np.float64), wt.astype(np.float64), dy.astype(np.float64), dyt.astype(np.float64)
    dx = np.zeros((N, 128, 128)); dw = np.zeros((N, 128, 128))
    for r in range(N):
        for j in range(N):
            dx[r] += WT[j].T @ DY[j][:, 128 * r:128 * r + 128]
            dw[r] += X[j].T @ DYT[r][:, 128 * j:128 * j + 128]
    return {"dx": dx.astype(np.float32 if x.dtype != np.float64 else np.float64), "dw": dw.astype(np.float32 if x.dtype != np.float64 else np.float64)}

@@ -1,0 +1,239 @@
+from concourse.bass import DstId, RemoteDMATransfer
+from concourse.mybir import AluOpType
+
+B = 128
+NR = 12
+NP = NR // 2
+
+SCRATCH = {
+    "xd": ("dram", [B, B], "float32"),
+    "hxd": ("dram", [B, B], "float32"),
+    "hp": ("sbuf", [B, 2 * B], "float32"),
+    "wts": ("sbuf", [B, B], "float32"),
+    "dys": ("sbuf", [B, NR * B], "float32"),
+    "dyts": ("sbuf", [B, NR * B], "float32"),
+    "psb": ("sbuf", [B, NR * B], "float32"),
+    "xall": ("sbuf", [B, NR * B], "float32"),
+    "pland": ("sbuf", [B, NR * B], "float32"),
+    "dxo": ("sbuf", [B, B], "float32"),
+    "dwo": ("sbuf", [B, B], "float32"),
+    "pw": ("psum", [B, 512], "float32"),
+}
+for _i in range(NP):
+    SCRATCH["pp%d" % _i] = ("psum", [B, 512], "float32")
+
+SEMAPHORES = (["ld_x", "ld_xd", "ld_wt", "mmw", "vch", "dx_done", "dw_done", "st_dx", "st_dw", "lsem", "hxs", "hps"]
+              + ["ld_dy%d" % i for i in range(NP)] + ["ld_dyt%d" % i for i in range(3)]
+              + ["mm%d" % i for i in range(NP)] + ["cp%d" % i for i in range(NP)]
+              + ["xs%d" % i for i in range(NP)] + ["ps%d" % i for i in range(NP)]
+              + ["gate%d" % i for i in range(3)])
+
+
+def _sub(mask, k, n):
+    bits = [b for b in range(mask.bit_length()) if (mask >> b) & 1][k:k + n]
+    m = 0
+    for b in bits:
+        m |= 1 << b
+    return m
+
+
+def _count(mask):
+    return len([b for b in range(mask.bit_length()) if (mask >> b) & 1])
+
+
+def _plan(T, topo):
+    cores = list(T.cores)
+    plane_a = [m for m in range(NP) if m == 0 or topo.same_plane(cores[0], cores[2 * m])]
+    plane_b = [m for m in range(NP) if m not in plane_a]
+    ranks, helpers = [], {}
+    for j, c in enumerate(cores):
+        mo = j // 2
+        mine, other = (plane_a, plane_b) if mo in plane_a else (plane_b, plane_a)
+        u = mine.index(mo)
+        cross = [other[(u + t) % len(other)] for t in range(len(other))]
+        same = [mine[(u + t) % len(mine)] for t in range(1, len(mine))]
+        k = topo.CORES_PER_CHIP
+        chipc = [h for h in range(max(0, c - k + 1), c + k)
+                 if h != c and topo.host(h) == topo.host(c) and topo.chip(h) == topo.chip(c)]
+        far = cores[2 * cross[0]]
+        port = [h for h in chipc if topo.may_write(h, far)]
+        plain = [h for h in chipc if h not in port]
+        port = [h for h in port if topo.die(h) == topo.die(c)] + [h for h in port if topo.die(h) != topo.die(c)]
+        plain = [h for h in plain if topo.die(h) == topo.die(c)] + [h for h in plain if topo.die(h) != topo.die(c)]
+        twin = 2 * mo + 1 - (j - 2 * mo)
+        steps = []
+        for t, m in enumerate(cross):
+            steps.append((m, [port[t]]))
+            helpers[port[t]] = {"rank": j, "xd": [2 * m, 2 * m + 1], "pd": [2 * m, 2 * m + 1]}
+        for s, m in enumerate(same):
+            hs = [plain[2 * s], plain[2 * s + 1]]
+            steps.append((m, hs))
+            for i, h in enumerate(hs):
+                helpers[h] = {"rank": j, "xd": [2 * m + i], "pd": [2 * m + i]}
+        helpers[plain[0]]["xd"].append(twin)
+        ranks.append({"mo": mo, "twin": twin, "steps": steps, "cross": cross, "same": same,
+                      "helpers": port[:len(cross)] + plain[:2 * len(same)]})
+    return {"cores": cores, "ranks": ranks, "helpers": helpers}
+
+
+def _dst(topo, d, src):
+    rid, pid = topo.addr(d, src)
+    return DstId(rid=rid, pnc=pid)
+
+
+def _blk(j):
+    return slice(j * B, (j + 1) * B)
+
+
+def _pair(m):
+    return slice(2 * m * B, (2 * m + 2) * B)
+
+
+def _helper(g, core, role, T, topo, plan):
+    S, cores, j = T.sem, plan["cores"], role["rank"]
+    m = j // 2
+    xd, pd = role["xd"], role["pd"]
+    mask = topo.mask(core, cores[xd[0]])
+    for d in xd + pd:
+        mask &= topo.mask(core, cores[d])
+    ne = _count(mask)
+    g.wait_ge(S.hxs, _count(topo.mask(cores[j], core)))
+    g.remote_dma_fused([RemoteDMATransfer(
+        dst_ids=[_dst(topo, cores[d], core) for d in xd], dma_engine_mask=mask, remote_sem=S["xs%d" % m],
+        srcs=[T.hxd[:]], dsts=[T.xall[:, _blk(j)] for d in xd])], local_sem=S.lsem)
+    g.wait_ge(S.hps, _count(topo.mask(cores[j], core)) // (3 - len(pd)))
+    per = ne // len(pd)
+    g.remote_dma_fused([RemoteDMATransfer(
+        dst_ids=[_dst(topo, cores[d], core)], dma_engine_mask=_sub(mask, i * per, per), remote_sem=S["ps%d" % m],
+        srcs=[T.hp[:, _blk(i)]], dsts=[T.pland[:, _blk(j)]]) for i, d in enumerate(pd)], local_sem=S.lsem)
+    g.wait_ge(S.lsem, 2 * ne)
+
+
+def _rank(g, core, r, T, topo, plan):
+    S, cores, me = T.sem, plan["cores"], plan["ranks"][r]
+    mo, twin, steps = me["mo"], me["twin"], me["steps"]
+    sy, sc, pe, v = g.sync, g.scalar, g.tensor, g.vector
+    order = [m for m, hs in steps] + [mo]
+    ns = len(steps)
+    dworder = [mo] + me["same"] + me["cross"]
+    pieces = []
+    for m in dworder:
+        if m // 2 not in pieces:
+            pieces.append(m // 2)
+
+    def ld_dy(q, i):
+        q.dma_start(T.dys[:, _pair(order[i])], T.dy[:, _pair(order[i])]).then_inc(S["ld_dy%d" % i], 16)
+
+    def ld_dyt(q, k):
+        p = pieces[k]
+        q.dma_start(T.dyts[:, 4 * p * B:(4 * p + 4) * B], T.dyt[:, 4 * p * B:(4 * p + 4) * B]).then_inc(S["ld_dyt%d" % p], 16)
+
+    sy.dma_start(T.xd[:], T.x[:]).then_inc(S.ld_xd, 16)
+    sc.dma_start(T.dys[:, _pair(order[0])], T.dy[:, _pair(order[0])]).then_inc(S.ld_dy0, 16)
+    sy.dma_start(T.wts[:], T.wt[:]).then_inc(S.ld_wt, 16)
+    ld_dy(sc, 2)
+    ld_dy(sy, 1)
+    ld_dy(sy, 3)
+    sc.wait_ge(S.ld_xd, 16)
+    ld_dy(sc, 4)
+    sy.wait_ge(S.ld_xd, 16)
+    ld_dy(sy, 5)
+    sc.dma_start(T.xall[:, _blk(r)], T.x[:]).then_inc(S.ld_x, 16)
+    sc.wait_ge(S.gate0, 1)
+    ld_dyt(sc, 0)
+    sy.wait_ge(S.gate1, 1)
+    ld_dyt(sy, 1)
+    sc.wait_ge(S.gate2, 1)
+    ld_dyt(sc, 2)
+
+    pe.wait_ge(S.ld_wt, 16)
+    for i, m in enumerate(order):
+        pe.wait_ge(S["ld_dy%d" % i], 16)
+        pe.matmul(T["pp%d" % i][:, 0:2 * B], T.wts[:], T.dys[:, _pair(m)], True, True).then_inc(S["mm%d" % i], 1)
+    off = _count(topo.mask(core, cores[twin]))
+    seq = [r, twin] + [j for m in dworder[1:] for j in (2 * m, 2 * m + 1)]
+    for n, j in enumerate(seq):
+        pe.wait_ge(S["ld_dyt%d" % (j // 4)], 16)
+        if j == r:
+            pe.wait_ge(S.ld_x, 16)
+        elif j == twin:
+            pe.wait_ge(S["xs%d" % mo], off)
+        else:
+            pe.wait_ge(S["xs%d" % (j // 2)], 2 * off)
+        ins = pe.matmul(T.pw[:, 0:B], T.xall[:, _blk(j)], T.dyts[:, _blk(j)], n == 0, n == len(seq) - 1)
+        if n == len(seq) - 1:
+            ins.then_inc(S.mmw, 1)
+
+    for i in range(ns):
+        v.wait_ge(S["mm%d" % i], 1)
+        v.tensor_copy(T.psb[:, _pair(order[i])], T["pp%d" % i][:, 0:2 * B]).then_inc(S["cp%d" % i], 1)
+    own_bank = T["pp%d" % ns]
+    v.wait_ge(S["mm%d" % ns], 1)
+    v.tensor_copy(T.psb[:, _blk(twin)], own_bank[:, _blk(twin - 2 * mo)]).then_inc(S["cp%d" % ns], 1)
+    acc = own_bank[:, _blk(r - 2 * mo)]
+    src_pairs = sorted([m for m in range(NP) if m != mo],
+                       key=lambda m: [p for p, hs in plan["ranks"][2 * m]["steps"]].index(mo))
+    groups = [([2 * m, 2 * m + 1], "ps%d" % m, off if m in me["cross"] else 2 * off) for m in src_pairs]
+    groups.insert(len(groups) - 1, ([twin], "ps%d" % mo, off))
+    k, total = 0, NR - 1
+    for srcs, sem, cnt in groups:
+        v.wait_ge(S[sem], cnt)
+        for s in srcs:
+            if k:
+                v.wait_ge(S.vch, k)
+            k += 1
+            last = k == total
+            v.tensor_tensor(T.dxo[:] if last else acc, acc, T.pland[:, _blk(s)], AluOpType.add).then_inc(
+                S.dx_done if last else S.vch, 1)
+    v.wait_ge(S.mmw, 1)
+    v.tensor_copy(T.dwo[:], T.pw[:, 0:B]).then_inc(S.dw_done, 1)
+
+    hs_all = me["helpers"]
+    on = topo.mask(core, hs_all[0])
+    for h in hs_all:
+        on &= topo.mask(core, h)
+    non = _count(on)
+    sent = 0
+    g.wait_ge(S.ld_xd, 16)
+    g.remote_dma_fused([RemoteDMATransfer(
+        dst_ids=[_dst(topo, h, core) for h in hs_all], dma_engine_mask=on, remote_sem=S.hxs,
+        srcs=[T.xd[:]], dsts=[T.hxd[:] for h in hs_all])], local_sem=S.lsem)
+    sent += non
+    g.sem_inc(S.gate0, 1)
+    for i, (m, hs) in enumerate(steps):
+        g.wait_ge(S["cp%d" % i], 1)
+        if len(hs) == 1:
+            rid, pid = topo.addr(hs[0], core)
+            g.remote_dma(T.hp[:, 0:2 * B], T.psb[:, _pair(m)], S.hps, S.lsem, pid, rid, on)
+        else:
+            per = non // len(hs)
+            g.remote_dma_fused([RemoteDMATransfer(
+                dst_ids=[_dst(topo, h, core)], dma_engine_mask=_sub(on, a * per, per), remote_sem=S.hps,
+                srcs=[T.psb[:, _blk(2 * m + a)]], dsts=[T.hp[:, 0:B]]) for a, h in enumerate(hs)], local_sem=S.lsem)
+        sent += non
+        if i == 1:
+            g.sem_inc(S.gate1, 1)
+        if i == 3:
+            g.sem_inc(S.gate2, 1)
+    g.wait_ge(S["cp%d" % ns], 1)
+    rid, pid = topo.addr(cores[twin], core)
+    g.remote_dma(T.pland[:, _blk(r)], T.psb[:, _blk(twin)], S["ps%d" % mo], S.lsem, pid, rid,
+                 topo.mask(core, cores[twin]))
+    sent += off
+    g.wait_ge(S.lsem, sent)
+
+    sy.wait_ge(S.dx_done, 1)
+    sy.dma_start(T.dx[:], T.dxo[:]).then_inc(S.st_dx, 16)
+    sy.wait_ge(S.st_dx, 16)
+    sc.wait_ge(S.dw_done, 1)
+    sc.dma_start(T.dw[:], T.dwo[:]).then_inc(S.st_dw, 16)
+    sc.wait_ge(S.st_dw, 16)
+
+
+def rank_program(g, core, T, topo):
+    plan = _plan(T, topo)
+    r = T.rank_of(core)
+    if r is not None:
+        _rank(g, core, r, T, topo, plan)
+    elif core in plan["helpers"]:
+        _helper(g, core, plan["helpers"][core], T, topo, plan)

@@ -9,12 +9,15 @@ SCRATCH = {
     "xd": ("dram", [B, B], "float32"),
     "hxd": ("dram", [B, B], "float32"),
     "hp": ("sbuf", [B, 2 * B], "float32"),
-    "wts": ("sbuf", [B, B], "float32"),
+    "sl": ("sbuf", [B, 5 * B], "float32"),
+    "hs": ("sbuf", [B, 3 * B], "float32"),
     "dys": ("sbuf", [B, NR * B], "float32"),
     "dyts": ("sbuf", [B, NR * B], "float32"),
     "psb": ("sbuf", [B, NR * B], "float32"),
     "xall": ("sbuf", [B, NR * B], "float32"),
     "pland": ("sbuf", [B, NR * B], "float32"),
+    "dwp": ("sbuf", [B, B], "float32"),
+    "tmp": ("sbuf", [B, B], "float32"),
     "dxo": ("sbuf", [B, B], "float32"),
     "dwo": ("sbuf", [B, B], "float32"),
     "pw": ("psum", [B, 512], "float32"),
@@ -22,10 +25,11 @@ SCRATCH = {
 for _i in range(NP):
     SCRATCH["pp%d" % _i] = ("psum", [B, 512], "float32")
 
-SEMAPHORES = (["ld_x", "ld_xd", "ld_wt", "mmw", "vch", "dx_done", "dw_done", "st_dx", "st_dw", "lsem", "hxs", "hps"]
+SEMAPHORES = (["ld_x", "ld_xd", "ld_wt", "mmw", "vc0", "vc1", "dx_done", "dw_done", "st_dx", "st_dw", "lsem", "hxs", "hps",
+               "hts", "dws"]
               + ["ld_dy%d" % i for i in range(NP)] + ["ld_dyt%d" % i for i in range(3)]
               + ["mm%d" % i for i in range(NP)] + ["cp%d" % i for i in range(NP)]
-              + ["xs%d" % i for i in range(NP)] + ["ps%d" % i for i in range(NP)]
+              + ["xs%d" % i for i in range(NR)] + ["ps%d" % i for i in range(NP)]
               + ["gate%d" % i for i in range(3)])
 
 
@@ -61,18 +65,16 @@ def _plan(T, topo):
         port = [h for h in port if topo.die(h) == topo.die(c)] + [h for h in port if topo.die(h) != topo.die(c)]
         plain = [h for h in plain if topo.die(h) == topo.die(c)] + [h for h in plain if topo.die(h) != topo.die(c)]
         twin = 2 * mo + 1 - (j - 2 * mo)
-        steps = []
         for t, m in enumerate(cross):
-            steps.append((m, [port[t]]))
-            helpers[port[t]] = {"rank": j, "xd": [2 * m, 2 * m + 1], "pd": [2 * m, 2 * m + 1]}
+            helpers[port[t]] = {"rank": j, "xd": [2 * m + j % 2, 2 * m + 1 - j % 2], "pd": [2 * m, 2 * m + 1],
+                                "mate": True, "dw": False, "comp": t if t < 2 else None}
         for s, m in enumerate(same):
-            hs = [plain[2 * s], plain[2 * s + 1]]
-            steps.append((m, hs))
-            for i, h in enumerate(hs):
-                helpers[h] = {"rank": j, "xd": [2 * m + i], "pd": [2 * m + i]}
+            for i, h in enumerate([plain[2 * s], plain[2 * s + 1]]):
+                helpers[h] = {"rank": j, "xd": [2 * m + i], "pd": [2 * m + i], "mate": False, "dw": False, "comp": None}
         helpers[plain[0]]["xd"].append(twin)
-        ranks.append({"mo": mo, "twin": twin, "steps": steps, "cross": cross, "same": same,
-                      "helpers": port[:len(cross)] + plain[:2 * len(same)]})
+        helpers[plain[1]]["dw"] = True
+        ranks.append({"mo": mo, "twin": twin, "cross": cross, "same": same, "port": port[:len(cross)],
+                      "plain": plain[:2 * len(same)], "dcore": plain[1]})
     return {"cores": cores, "ranks": ranks, "helpers": helpers}
 
 
@@ -89,77 +91,108 @@ def _pair(m):
     return slice(2 * m * B, (2 * m + 2) * B)
 
 
+def _back(topo, plan, j):
+    d = plan["ranks"][j]["dcore"]
+    return topo.mask(d, plan["cores"][j]) & topo.mask(d, plan["cores"][plan["ranks"][j]["twin"]])
+
+
 def _helper(g, core, role, T, topo, plan):
     S, cores, j = T.sem, plan["cores"], role["rank"]
+    me = plan["ranks"][j]
     m = j // 2
     xd, pd = role["xd"], role["pd"]
-    mask = topo.mask(core, cores[xd[0]])
-    for d in xd + pd:
-        mask &= topo.mask(core, cores[d])
+    pe, v = g.tensor, g.vector
+    xc = [cores[d] if (role["mate"] or d == me["twin"]) else plan["ranks"][d]["dcore"] for d in xd]
+    mask = topo.mask(core, xc[0])
+    for t in xc + [cores[d] for d in pd]:
+        mask &= topo.mask(core, t)
     ne = _count(mask)
-    g.wait_ge(S.hxs, _count(topo.mask(cores[j], core)))
+    non = _count(topo.mask(cores[j], core))
+    sent = 0
+    g.wait_ge(S.hxs, non)
     g.remote_dma_fused([RemoteDMATransfer(
-        dst_ids=[_dst(topo, cores[d], core) for d in xd], dma_engine_mask=mask, remote_sem=S["xs%d" % m],
-        srcs=[T.hxd[:]], dsts=[T.xall[:, _blk(j)] for d in xd])], local_sem=S.lsem)
-    g.wait_ge(S.hps, _count(topo.mask(cores[j], core)) // (3 - len(pd)))
+        dst_ids=[_dst(topo, t, core) for t in xc], dma_engine_mask=mask, remote_sem=S["xs%d" % j],
+        srcs=[T.hxd[:]], dsts=[T.xall[:, _blk(j)] for t in xc])], local_sem=S.lsem)
+    sent += ne
+    if role["comp"] is not None:
+        w0, d0 = (2 * B, 0) if role["comp"] == 0 else (0, B)
+        pe.wait_ge(S.hps, non // 2)
+        pe.matmul(T.pp0[:, 0:2 * B], T.hs[:, w0:w0 + B], T.hs[:, d0:d0 + 2 * B], True, True).then_inc(S.mm0, 1)
+        v.wait_ge(S.mm0, 1)
+        v.tensor_copy(T.hp[:, 0:2 * B], T.pp0[:, 0:2 * B]).then_inc(S.cp0, 1)
+        g.wait_ge(S.cp0, 1)
+    else:
+        g.wait_ge(S.hps, non // (3 - len(pd)))
     per = ne // len(pd)
     g.remote_dma_fused([RemoteDMATransfer(
         dst_ids=[_dst(topo, cores[d], core)], dma_engine_mask=_sub(mask, i * per, per), remote_sem=S["ps%d" % m],
         srcs=[T.hp[:, _blk(i)]], dsts=[T.pland[:, _blk(j)]]) for i, d in enumerate(pd)], local_sem=S.lsem)
-    g.wait_ge(S.lsem, 2 * ne)
+    sent += ne
+    if role["dw"]:
+        srcs = [s for p in me["same"] for s in (2 * p, 2 * p + 1)]
+        pe.wait_ge(S.hts, non)
+        for n, s in enumerate(srcs):
+            pe.wait_ge(S["xs%d" % s], ne)
+            ins = pe.matmul(T.pw[:, 0:B], T.xall[:, _blk(s)], T.dyts[:, _blk(s)], n == 0, n == len(srcs) - 1)
+            if n == len(srcs) - 1:
+                ins.then_inc(S.mmw, 1)
+        v.wait_ge(S.mmw, 1)
+        v.tensor_copy(T.dwo[:], T.pw[:, 0:B]).then_inc(S.dw_done, 1)
+        g.wait_ge(S.dw_done, 1)
+        rid, pid = topo.addr(cores[j], core)
+        back = _back(topo, plan, j)
+        g.remote_dma(T.dwp[:], T.dwo[:], S.dws, S.lsem, pid, rid, back)
+        sent += _count(back)
+    g.wait_ge(S.lsem, sent)
 
 
 def _rank(g, core, r, T, topo, plan):
     S, cores, me = T.sem, plan["cores"], plan["ranks"][r]
-    mo, twin, steps = me["mo"], me["twin"], me["steps"]
+    mo, twin, cross, same = me["mo"], me["twin"], me["cross"], me["same"]
     sy, sc, pe, v = g.sync, g.scalar, g.tensor, g.vector
-    order = [m for m, hs in steps] + [mo]
-    ns = len(steps)
-    dworder = [mo] + me["same"] + me["cross"]
-    pieces = []
-    for m in dworder:
-        if m // 2 not in pieces:
-            pieces.append(m // 2)
+    order = same + [cross[2], mo]
+    ns = len(order) - 1
+    wts = T.sl[:, 2 * B:3 * B]
 
-    def ld_dy(q, i):
-        q.dma_start(T.dys[:, _pair(order[i])], T.dy[:, _pair(order[i])]).then_inc(S["ld_dy%d" % i], 16)
+    def ld_dy(q, m):
+        q.dma_start(T.dys[:, _pair(m)], T.dy[:, _pair(m)]).then_inc(S["ld_dy%d" % m], 16)
 
-    def ld_dyt(q, k):
-        p = pieces[k]
+    def ld_sl(q, m, c):
+        q.dma_start(T.sl[:, c:c + 2 * B], T.dy[:, _pair(m)]).then_inc(S["ld_dy%d" % m], 16)
+
+    def ld_dyt(q, p):
         q.dma_start(T.dyts[:, 4 * p * B:(4 * p + 4) * B], T.dyt[:, 4 * p * B:(4 * p + 4) * B]).then_inc(S["ld_dyt%d" % p], 16)
 
     sy.dma_start(T.xd[:], T.x[:]).then_inc(S.ld_xd, 16)
-    sc.dma_start(T.dys[:, _pair(order[0])], T.dy[:, _pair(order[0])]).then_inc(S.ld_dy0, 16)
-    sy.dma_start(T.wts[:], T.wt[:]).then_inc(S.ld_wt, 16)
-    ld_dy(sc, 2)
-    ld_dy(sy, 1)
-    ld_dy(sy, 3)
-    sc.wait_ge(S.ld_xd, 16)
-    ld_dy(sc, 4)
+    sc.dma_start(wts, T.wt[:]).then_inc(S.ld_wt, 16)
+    ld_dy(sy, same[0])
+    ld_sl(sc, cross[0], 0)
+    ld_sl(sy, cross[1], 3 * B)
+    ld_dy(sc, same[1])
     sy.wait_ge(S.ld_xd, 16)
-    ld_dy(sy, 5)
+    ld_dy(sy, cross[2])
+    sc.wait_ge(S.ld_xd, 16)
+    ld_dy(sc, mo)
     sc.dma_start(T.xall[:, _blk(r)], T.x[:]).then_inc(S.ld_x, 16)
-    sc.wait_ge(S.gate0, 1)
-    ld_dyt(sc, 0)
-    sy.wait_ge(S.gate1, 1)
-    ld_dyt(sy, 1)
-    sc.wait_ge(S.gate2, 1)
-    ld_dyt(sc, 2)
+    sy.wait_ge(S.gate0, 1)
+    ld_dyt(sy, same[0] // 2)
+    sc.wait_ge(S.gate1, 1)
+    ld_dyt(sc, same[1] // 2)
+    sy.wait_ge(S.gate2, 1)
+    ld_dyt(sy, mo // 2)
 
     pe.wait_ge(S.ld_wt, 16)
     for i, m in enumerate(order):
-        pe.wait_ge(S["ld_dy%d" % i], 16)
-        pe.matmul(T["pp%d" % i][:, 0:2 * B], T.wts[:], T.dys[:, _pair(m)], True, True).then_inc(S["mm%d" % i], 1)
+        pe.wait_ge(S["ld_dy%d" % m], 16)
+        pe.matmul(T["pp%d" % i][:, 0:2 * B], wts, T.dys[:, _pair(m)], True, True).then_inc(S["mm%d" % i], 1)
     off = _count(topo.mask(core, cores[twin]))
-    seq = [r, twin] + [j for m in dworder[1:] for j in (2 * m, 2 * m + 1)]
+    seq = [r, twin] + [2 * m + r % 2 for m in cross] + [2 * m + 1 - r % 2 for m in cross]
     for n, j in enumerate(seq):
         pe.wait_ge(S["ld_dyt%d" % (j // 4)], 16)
         if j == r:
             pe.wait_ge(S.ld_x, 16)
-        elif j == twin:
-            pe.wait_ge(S["xs%d" % mo], off)
         else:
-            pe.wait_ge(S["xs%d" % (j // 2)], 2 * off)
+            pe.wait_ge(S["xs%d" % j], off)
         ins = pe.matmul(T.pw[:, 0:B], T.xall[:, _blk(j)], T.dyts[:, _blk(j)], n == 0, n == len(seq) - 1)
         if n == len(seq) - 1:
             ins.then_inc(S.mmw, 1)
@@ -171,24 +204,44 @@ def _rank(g, core, r, T, topo, plan):
     v.wait_ge(S["mm%d" % ns], 1)
     v.tensor_copy(T.psb[:, _blk(twin)], own_bank[:, _blk(twin - 2 * mo)]).then_inc(S["cp%d" % ns], 1)
     acc = own_bank[:, _blk(r - 2 * mo)]
-    src_pairs = sorted([m for m in range(NP) if m != mo],
-                       key=lambda m: [p for p, hs in plan["ranks"][2 * m]["steps"]].index(mo))
-    groups = [([2 * m, 2 * m + 1], "ps%d" % m, off if m in me["cross"] else 2 * off) for m in src_pairs]
-    groups.insert(len(groups) - 1, ([twin], "ps%d" % mo, off))
-    k, total = 0, NR - 1
-    for srcs, sem, cnt in groups:
-        v.wait_ge(S[sem], cnt)
-        for s in srcs:
-            if k:
-                v.wait_ge(S.vch, k)
-            k += 1
-            last = k == total
-            v.tensor_tensor(T.dxo[:] if last else acc, acc, T.pland[:, _blk(s)], AluOpType.add).then_inc(
-                S.dx_done if last else S.vch, 1)
-    v.wait_ge(S.mmw, 1)
-    v.tensor_copy(T.dwo[:], T.pw[:, 0:B]).then_inc(S.dw_done, 1)
+    near = sorted(same, key=lambda m: plan["ranks"][2 * m]["same"].index(mo))
+    far = sorted(cross, key=lambda m: plan["ranks"][2 * m]["cross"].index(mo))
+    acc1 = T["pp%d" % (ns + 1)][:, 0:B]
+    cnt = {"vc0": 0, "vc1": 0}
 
-    hs_all = me["helpers"]
+    def add(out, a, s, deps, sem):
+        for d in deps:
+            if cnt[d]:
+                v.wait_ge(S[d], cnt[d])
+        v.tensor_tensor(out, a, s, AluOpType.add).then_inc(S[sem], 1)
+        if sem in cnt:
+            cnt[sem] += 1
+
+    def land(s):
+        return T.pland[:, _blk(s)]
+
+    v.wait_ge(S["ps%d" % near[0]], 2 * off)
+    add(acc, acc, land(2 * near[0]), ["vc0"], "vc0")
+    v.wait_ge(S["ps%d" % near[1]], 2 * off)
+    add(acc1, land(2 * near[0] + 1), land(2 * near[1] + 1), [], "vc1")
+    add(acc, acc, land(2 * near[1]), ["vc0"], "vc0")
+    v.wait_ge(S["ps%d" % mo], off)
+    add(acc1, acc1, land(twin), ["vc1"], "vc1")
+    v.wait_ge(S["ps%d" % far[0]], off)
+    add(acc, acc, land(2 * far[0]), ["vc0"], "vc0")
+    add(acc1, acc1, land(2 * far[0] + 1), ["vc1"], "vc1")
+    v.wait_ge(S["ps%d" % far[1]], off)
+    add(acc, acc, land(2 * far[1]), ["vc0"], "vc0")
+    add(T.tmp[:], acc1, land(2 * far[1] + 1), ["vc1"], "vc1")
+    add(acc, acc, T.tmp[:], ["vc0", "vc1"], "vc0")
+    v.wait_ge(S["ps%d" % far[2]], off)
+    add(acc, acc, land(2 * far[2]), ["vc0"], "vc0")
+    add(T.dxo[:], acc, land(2 * far[2] + 1), ["vc0"], "dx_done")
+    v.wait_ge(S.mmw, 1)
+    v.wait_ge(S.dws, _count(_back(topo, plan, r)))
+    v.tensor_tensor(T.dwo[:], T.pw[:, 0:B], T.dwp[:], AluOpType.add).then_inc(S.dw_done, 1)
+
+    hs_all = me["port"] + me["plain"]
     on = topo.mask(core, hs_all[0])
     for h in hs_all:
         on &= topo.mask(core, h)
@@ -199,27 +252,38 @@ def _rank(g, core, r, T, topo, plan):
         dst_ids=[_dst(topo, h, core) for h in hs_all], dma_engine_mask=on, remote_sem=S.hxs,
         srcs=[T.xd[:]], dsts=[T.hxd[:] for h in hs_all])], local_sem=S.lsem)
     sent += non
+    per = non // 2
+    g.wait_ge(S.ld_wt, 16)
+    g.wait_ge(S["ld_dy%d" % cross[0]], 16)
+    g.wait_ge(S["ld_dy%d" % cross[1]], 16)
+    g.remote_dma_fused([RemoteDMATransfer(
+        dst_ids=[_dst(topo, me["port"][a], core)], dma_engine_mask=_sub(on, a * per, per), remote_sem=S.hps,
+        srcs=[T.sl[:, 2 * a * B:(2 * a + 3) * B]], dsts=[T.hs[:]]) for a in range(2)], local_sem=S.lsem)
+    sent += non
     g.sem_inc(S.gate0, 1)
-    for i, (m, hs) in enumerate(steps):
+    for i, m in enumerate(same):
+        hs = [me["plain"][2 * i], me["plain"][2 * i + 1]]
         g.wait_ge(S["cp%d" % i], 1)
-        if len(hs) == 1:
-            rid, pid = topo.addr(hs[0], core)
-            g.remote_dma(T.hp[:, 0:2 * B], T.psb[:, _pair(m)], S.hps, S.lsem, pid, rid, on)
-        else:
-            per = non // len(hs)
-            g.remote_dma_fused([RemoteDMATransfer(
-                dst_ids=[_dst(topo, h, core)], dma_engine_mask=_sub(on, a * per, per), remote_sem=S.hps,
-                srcs=[T.psb[:, _blk(2 * m + a)]], dsts=[T.hp[:, 0:B]]) for a, h in enumerate(hs)], local_sem=S.lsem)
+        g.remote_dma_fused([RemoteDMATransfer(
+            dst_ids=[_dst(topo, h, core)], dma_engine_mask=_sub(on, a * per, per), remote_sem=S.hps,
+            srcs=[T.psb[:, _blk(2 * m + a)]], dsts=[T.hp[:, 0:B]]) for a, h in enumerate(hs)], local_sem=S.lsem)
         sent += non
-        if i == 1:
-            g.sem_inc(S.gate1, 1)
-        if i == 3:
-            g.sem_inc(S.gate2, 1)
+        g.sem_inc(S["gate%d" % (i + 1)], 1)
+    g.wait_ge(S["cp%d" % len(same)], 1)
+    rid, pid = topo.addr(me["port"][2], core)
+    g.remote_dma(T.hp[:, 0:2 * B], T.psb[:, _pair(cross[2])], S.hps, S.lsem, pid, rid, on)
+    sent += non
     g.wait_ge(S["cp%d" % ns], 1)
     rid, pid = topo.addr(cores[twin], core)
     g.remote_dma(T.pland[:, _blk(r)], T.psb[:, _blk(twin)], S["ps%d" % mo], S.lsem, pid, rid,
                  topo.mask(core, cores[twin]))
     sent += off
+    for m in same:
+        g.wait_ge(S["ld_dyt%d" % (m // 2)], 16)
+    g.remote_dma_fused([RemoteDMATransfer(
+        dst_ids=[_dst(topo, me["dcore"], core)], dma_engine_mask=_sub(on, a * per, per), remote_sem=S.hts,
+        srcs=[T.dyts[:, _pair(m)]], dsts=[T.dyts[:, _pair(m)]]) for a, m in enumerate(same)], local_sem=S.lsem)
+    sent += non
     g.wait_ge(S.lsem, sent)
 
     sy.wait_ge(S.dx_done, 1)

from concourse.bass import DstId, RemoteDMATransfer
from concourse.mybir import AluOpType

B = 128
NR = 12
NP = NR // 2

SCRATCH = {
    "xd": ("dram", [B, B], "float32"),
    "hxd": ("dram", [B, B], "float32"),
    "hp": ("sbuf", [B, 2 * B], "float32"),
    "sl": ("sbuf", [B, 5 * B], "float32"),
    "hs": ("sbuf", [B, 3 * B], "float32"),
    "dys": ("sbuf", [B, NR * B], "float32"),
    "dyts": ("sbuf", [B, NR * B], "float32"),
    "psb": ("sbuf", [B, NR * B], "float32"),
    "xall": ("sbuf", [B, NR * B], "float32"),
    "pland": ("sbuf", [B, NR * B], "float32"),
    "dwp": ("sbuf", [B, B], "float32"),
    "tmp": ("sbuf", [B, B], "float32"),
    "dxo": ("sbuf", [B, B], "float32"),
    "dwo": ("sbuf", [B, B], "float32"),
    "pw": ("psum", [B, 512], "float32"),
}
for _i in range(NP):
    SCRATCH["pp%d" % _i] = ("psum", [B, 512], "float32")

SEMAPHORES = (["ld_x", "ld_xd", "ld_wt", "mmw", "vc0", "vc1", "dx_done", "dw_done", "st_dx", "st_dw", "lsem", "hxs", "hps",
               "hts", "dws"]
              + ["ld_dy%d" % i for i in range(NP)] + ["ld_dyt%d" % i for i in range(3)]
              + ["mm%d" % i for i in range(NP)] + ["cp%d" % i for i in range(NP)]
              + ["xs%d" % i for i in range(NR)] + ["ps%d" % i for i in range(NP)]
              + ["gate%d" % i for i in range(3)])


def _sub(mask, k, n):
    bits = [b for b in range(mask.bit_length()) if (mask >> b) & 1][k:k + n]
    m = 0
    for b in bits:
        m |= 1 << b
    return m


def _count(mask):
    return len([b for b in range(mask.bit_length()) if (mask >> b) & 1])


def _plan(T, topo):
    cores = list(T.cores)
    plane_a = [m for m in range(NP) if m == 0 or topo.same_plane(cores[0], cores[2 * m])]
    plane_b = [m for m in range(NP) if m not in plane_a]
    ranks, helpers = [], {}
    for j, c in enumerate(cores):
        mo = j // 2
        mine, other = (plane_a, plane_b) if mo in plane_a else (plane_b, plane_a)
        u = mine.index(mo)
        cross = [other[(u + t) % len(other)] for t in range(len(other))]
        same = [mine[(u + t) % len(mine)] for t in range(1, len(mine))]
        k = topo.CORES_PER_CHIP
        chipc = [h for h in range(max(0, c - k + 1), c + k)
                 if h != c and topo.host(h) == topo.host(c) and topo.chip(h) == topo.chip(c)]
        far = cores[2 * cross[0]]
        port = [h for h in chipc if topo.may_write(h, far)]
        plain = [h for h in chipc if h not in port]
        port = [h for h in port if topo.die(h) == topo.die(c)] + [h for h in port if topo.die(h) != topo.die(c)]
        plain = [h for h in plain if topo.die(h) == topo.die(c)] + [h for h in plain if topo.die(h) != topo.die(c)]
        twin = 2 * mo + 1 - (j - 2 * mo)
        for t, m in enumerate(cross):
            helpers[port[t]] = {"rank": j, "xd": [2 * m + j % 2, 2 * m + 1 - j % 2], "pd": [2 * m, 2 * m + 1],
                                "mate": True, "dw": False, "comp": t if t < 2 else None}
        for s, m in enumerate(same):
            for i, h in enumerate([plain[2 * s], plain[2 * s + 1]]):
                helpers[h] = {"rank": j, "xd": [2 * m + i], "pd": [2 * m + i], "mate": False, "dw": False, "comp": None}
        helpers[plain[0]]["xd"].append(twin)
        helpers[plain[1]]["dw"] = True
        ranks.append({"mo": mo, "twin": twin, "cross": cross, "same": same, "port": port[:len(cross)],
                      "plain": plain[:2 * len(same)], "dcore": plain[1]})
    return {"cores": cores, "ranks": ranks, "helpers": helpers}


def _dst(topo, d, src):
    rid, pid = topo.addr(d, src)
    return DstId(rid=rid, pnc=pid)


def _blk(j):
    return slice(j * B, (j + 1) * B)


def _pair(m):
    return slice(2 * m * B, (2 * m + 2) * B)


def _back(topo, plan, j):
    d = plan["ranks"][j]["dcore"]
    return topo.mask(d, plan["cores"][j]) & topo.mask(d, plan["cores"][plan["ranks"][j]["twin"]])


def _helper(g, core, role, T, topo, plan):
    S, cores, j = T.sem, plan["cores"], role["rank"]
    me = plan["ranks"][j]
    m = j // 2
    xd, pd = role["xd"], role["pd"]
    pe, v = g.tensor, g.vector
    xc = [cores[d] if (role["mate"] or d == me["twin"]) else plan["ranks"][d]["dcore"] for d in xd]
    mask = topo.mask(core, xc[0])
    for t in xc + [cores[d] for d in pd]:
        mask &= topo.mask(core, t)
    ne = _count(mask)
    non = _count(topo.mask(cores[j], core))
    sent = 0
    g.wait_ge(S.hxs, non)
    g.remote_dma_fused([RemoteDMATransfer(
        dst_ids=[_dst(topo, t, core) for t in xc], dma_engine_mask=mask, remote_sem=S["xs%d" % j],
        srcs=[T.hxd[:]], dsts=[T.xall[:, _blk(j)] for t in xc])], local_sem=S.lsem)
    sent += ne
    if role["comp"] is not None:
        w0, d0 = (2 * B, 0) if role["comp"] == 0 else (0, B)
        pe.wait_ge(S.hps, non // 2)
        pe.matmul(T.pp0[:, 0:2 * B], T.hs[:, w0:w0 + B], T.hs[:, d0:d0 + 2 * B], True, True).then_inc(S.mm0, 1)
        v.wait_ge(S.mm0, 1)
        v.tensor_copy(T.hp[:, 0:2 * B], T.pp0[:, 0:2 * B]).then_inc(S.cp0, 1)
        g.wait_ge(S.cp0, 1)
    else:
        g.wait_ge(S.hps, non // (3 - len(pd)))
    per = ne // len(pd)
    g.remote_dma_fused([RemoteDMATransfer(
        dst_ids=[_dst(topo, cores[d], core)], dma_engine_mask=_sub(mask, i * per, per), remote_sem=S["ps%d" % m],
        srcs=[T.hp[:, _blk(i)]], dsts=[T.pland[:, _blk(j)]]) for i, d in enumerate(pd)], local_sem=S.lsem)
    sent += ne
    if role["dw"]:
        srcs = [s for p in me["same"] for s in (2 * p, 2 * p + 1)]
        pe.wait_ge(S.hts, non)
        for n, s in enumerate(srcs):
            pe.wait_ge(S["xs%d" % s], ne)
            ins = pe.matmul(T.pw[:, 0:B], T.xall[:, _blk(s)], T.dyts[:, _blk(s)], n == 0, n == len(srcs) - 1)
            if n == len(srcs) - 1:
                ins.then_inc(S.mmw, 1)
        v.wait_ge(S.mmw, 1)
        v.tensor_copy(T.dwo[:], T.pw[:, 0:B]).then_inc(S.dw_done, 1)
        g.wait_ge(S.dw_done, 1)
        rid, pid = topo.addr(cores[j], core)
        back = _back(topo, plan, j)
        g.remote_dma(T.dwp[:], T.dwo[:], S.dws, S.lsem, pid, rid, back)
        sent += _count(back)
    g.wait_ge(S.lsem, sent)


def _rank(g, core, r, T, topo, plan):
    S, cores, me = T.sem, plan["cores"], plan["ranks"][r]
    mo, twin, cross, same = me["mo"], me["twin"], me["cross"], me["same"]
    sy, sc, pe, v = g.sync, g.scalar, g.tensor, g.vector
    order = same + [cross[2], mo]
    ns = len(order) - 1
    wts = T.sl[:, 2 * B:3 * B]

    def ld_dy(q, m):
        q.dma_start(T.dys[:, _pair(m)], T.dy[:, _pair(m)]).then_inc(S["ld_dy%d" % m], 16)

    def ld_sl(q, m, c):
        q.dma_start(T.sl[:, c:c + 2 * B], T.dy[:, _pair(m)]).then_inc(S["ld_dy%d" % m], 16)

    def ld_dyt(q, p):
        q.dma_start(T.dyts[:, 4 * p * B:(4 * p + 4) * B], T.dyt[:, 4 * p * B:(4 * p + 4) * B]).then_inc(S["ld_dyt%d" % p], 16)

    sy.dma_start(T.xd[:], T.x[:]).then_inc(S.ld_xd, 16)
    sc.dma_start(wts, T.wt[:]).then_inc(S.ld_wt, 16)
    ld_dy(sy, same[0])
    ld_sl(sc, cross[0], 0)
    ld_sl(sy, cross[1], 3 * B)
    ld_dy(sc, same[1])
    sy.wait_ge(S.ld_xd, 16)
    ld_dy(sy, cross[2])
    sc.wait_ge(S.ld_xd, 16)
    ld_dy(sc, mo)
    sc.dma_start(T.xall[:, _blk(r)], T.x[:]).then_inc(S.ld_x, 16)
    sy.wait_ge(S.gate0, 1)
    ld_dyt(sy, same[0] // 2)
    sc.wait_ge(S.gate1, 1)
    ld_dyt(sc, same[1] // 2)
    sy.wait_ge(S.gate2, 1)
    ld_dyt(sy, mo // 2)

    pe.wait_ge(S.ld_wt, 16)
    for i, m in enumerate(order):
        pe.wait_ge(S["ld_dy%d" % m], 16)
        pe.matmul(T["pp%d" % i][:, 0:2 * B], wts, T.dys[:, _pair(m)], True, True).then_inc(S["mm%d" % i], 1)
    off = _count(topo.mask(core, cores[twin]))
    seq = [r, twin] + [2 * m + r % 2 for m in cross] + [2 * m + 1 - r % 2 for m in cross]
    for n, j in enumerate(seq):
        pe.wait_ge(S["ld_dyt%d" % (j // 4)], 16)
        if j == r:
            pe.wait_ge(S.ld_x, 16)
        else:
            pe.wait_ge(S["xs%d" % j], off)
        ins = pe.matmul(T.pw[:, 0:B], T.xall[:, _blk(j)], T.dyts[:, _blk(j)], n == 0, n == len(seq) - 1)
        if n == len(seq) - 1:
            ins.then_inc(S.mmw, 1)

    for i in range(ns):
        v.wait_ge(S["mm%d" % i], 1)
        v.tensor_copy(T.psb[:, _pair(order[i])], T["pp%d" % i][:, 0:2 * B]).then_inc(S["cp%d" % i], 1)
    own_bank = T["pp%d" % ns]
    v.wait_ge(S["mm%d" % ns], 1)
    v.tensor_copy(T.psb[:, _blk(twin)], own_bank[:, _blk(twin - 2 * mo)]).then_inc(S["cp%d" % ns], 1)
    acc = own_bank[:, _blk(r - 2 * mo)]
    near = sorted(same, key=lambda m: plan["ranks"][2 * m]["same"].index(mo))
    far = sorted(cross, key=lambda m: plan["ranks"][2 * m]["cross"].index(mo))
    acc1 = T["pp%d" % (ns + 1)][:, 0:B]
    cnt = {"vc0": 0, "vc1": 0}

    def add(out, a, s, deps, sem):
        for d in deps:
            if cnt[d]:
                v.wait_ge(S[d], cnt[d])
        v.tensor_tensor(out, a, s, AluOpType.add).then_inc(S[sem], 1)
        if sem in cnt:
            cnt[sem] += 1

    def land(s):
        return T.pland[:, _blk(s)]

    v.wait_ge(S["ps%d" % near[0]], 2 * off)
    add(acc, acc, land(2 * near[0]), ["vc0"], "vc0")
    v.wait_ge(S["ps%d" % near[1]], 2 * off)
    add(acc1, land(2 * near[0] + 1), land(2 * near[1] + 1), [], "vc1")
    add(acc, acc, land(2 * near[1]), ["vc0"], "vc0")
    v.wait_ge(S["ps%d" % mo], off)
    add(acc1, acc1, land(twin), ["vc1"], "vc1")
    v.wait_ge(S["ps%d" % far[0]], off)
    add(acc, acc, land(2 * far[0]), ["vc0"], "vc0")
    add(acc1, acc1, land(2 * far[0] + 1), ["vc1"], "vc1")
    v.wait_ge(S["ps%d" % far[1]], off)
    add(acc, acc, land(2 * far[1]), ["vc0"], "vc0")
    add(T.tmp[:], acc1, land(2 * far[1] + 1), ["vc1"], "vc1")
    add(acc, acc, T.tmp[:], ["vc0", "vc1"], "vc0")
    v.wait_ge(S["ps%d" % far[2]], off)
    add(acc, acc, land(2 * far[2]), ["vc0"], "vc0")
    add(T.dxo[:], acc, land(2 * far[2] + 1), ["vc0"], "dx_done")
    v.wait_ge(S.mmw, 1)
    v.wait_ge(S.dws, _count(_back(topo, plan, r)))
    v.tensor_tensor(T.dwo[:], T.pw[:, 0:B], T.dwp[:], AluOpType.add).then_inc(S.dw_done, 1)

    hs_all = me["port"] + me["plain"]
    on = topo.mask(core, hs_all[0])
    for h in hs_all:
        on &= topo.mask(core, h)
    non = _count(on)
    sent = 0
    g.wait_ge(S.ld_xd, 16)
    g.remote_dma_fused([RemoteDMATransfer(
        dst_ids=[_dst(topo, h, core) for h in hs_all], dma_engine_mask=on, remote_sem=S.hxs,
        srcs=[T.xd[:]], dsts=[T.hxd[:] for h in hs_all])], local_sem=S.lsem)
    sent += non
    per = non // 2
    g.wait_ge(S.ld_wt, 16)
    g.wait_ge(S["ld_dy%d" % cross[0]], 16)
    g.wait_ge(S["ld_dy%d" % cross[1]], 16)
    g.remote_dma_fused([RemoteDMATransfer(
        dst_ids=[_dst(topo, me["port"][a], core)], dma_engine_mask=_sub(on, a * per, per), remote_sem=S.hps,
        srcs=[T.sl[:, 2 * a * B:(2 * a + 3) * B]], dsts=[T.hs[:]]) for a in range(2)], local_sem=S.lsem)
    sent += non
    g.sem_inc(S.gate0, 1)
    for i, m in enumerate(same):
        hs = [me["plain"][2 * i], me["plain"][2 * i + 1]]
        g.wait_ge(S["cp%d" % i], 1)
        g.remote_dma_fused([RemoteDMATransfer(
            dst_ids=[_dst(topo, h, core)], dma_engine_mask=_sub(on, a * per, per), remote_sem=S.hps,
            srcs=[T.psb[:, _blk(2 * m + a)]], dsts=[T.hp[:, 0:B]]) for a, h in enumerate(hs)], local_sem=S.lsem)
        sent += non
        g.sem_inc(S["gate%d" % (i + 1)], 1)
    g.wait_ge(S["cp%d" % len(same)], 1)
    rid, pid = topo.addr(me["port"][2], core)
    g.remote_dma(T.hp[:, 0:2 * B], T.psb[:, _pair(cross[2])], S.hps, S.lsem, pid, rid, on)
    sent += non
    g.wait_ge(S["cp%d" % ns], 1)
    rid, pid = topo.addr(cores[twin], core)
    g.remote_dma(T.pland[:, _blk(r)], T.psb[:, _blk(twin)], S["ps%d" % mo], S.lsem, pid, rid,
                 topo.mask(core, cores[twin]))
    sent += off
    for m in same:
        g.wait_ge(S["ld_dyt%d" % (m // 2)], 16)
    g.remote_dma_fused([RemoteDMATransfer(
        dst_ids=[_dst(topo, me["dcore"], core)], dma_engine_mask=_sub(on, a * per, per), remote_sem=S.hts,
        srcs=[T.dyts[:, _pair(m)]], dsts=[T.dyts[:, _pair(m)]]) for a, m in enumerate(same)], local_sem=S.lsem)
    sent += non
    g.wait_ge(S.lsem, sent)

    sy.wait_ge(S.dx_done, 1)
    sy.dma_start(T.dx[:], T.dxo[:]).then_inc(S.st_dx, 16)
    sy.wait_ge(S.st_dx, 16)
    sc.wait_ge(S.dw_done, 1)
    sc.dma_start(T.dw[:], T.dwo[:]).then_inc(S.st_dw, 16)
    sc.wait_ge(S.st_dw, 16)


def rank_program(g, core, T, topo):
    plan = _plan(T, topo)
    r = T.rank_of(core)
    if r is not None:
        _rank(g, core, r, T, topo, plan)
    elif core in plan["helpers"]:
        _helper(g, core, plan["helpers"][core], T, topo, plan)
